import numpy as np, ml_dtypes
CORES = [9,17,137,145,265,273,393,401]
N = 8
import mx_ref
NC = 128
M = NC // N
BF = ml_dtypes.bfloat16
def cut(t, i, w=512):
    return t[:, w * i:w * i + w]
def term(a, B):
    return np.stack([mx_ref.matmul(mx_ref.quantize(cut(a, i)), B) for i in range(4)], axis=2).reshape(128, -1)
def setup_inputs(rng):
    def f(*shape):
        return mx_ref.flush((rng.standard_normal(shape, dtype=np.float32) * np.exp2(rng.integers(-2, 3, shape[:-1] + (1,)))).astype(BF))
    return {"a": f(N, 128, 4 * 512), "b": f(N, 128, 4 * NC)}
def setup_inputs_blocks(rng):
    d = setup_inputs(rng)
    for k in ("a", "b"): d[k] = mx_ref.spread(d[k], rng, 2)
    return d
def setup_inputs_wide(rng):
    d = setup_inputs(rng)
    for k in ("a", "b"): d[k] = mx_ref.flush((d[k].astype(np.float32) * np.exp2(rng.integers(-4, 5, (N, 1, 1))).astype(np.float32)).astype(BF))
    return d
def setup_inputs_lossless(rng):
    a = np.zeros((N, 128, 4 * 128, 4), np.float32)
    for r in range(N):
        k = rng.integers(0, 512, size=4 * 128)
        a[r, k // 4, np.arange(4 * 128), k % 4] = 1.0
    size = np.repeat(2.0 ** rng.integers(-4, 5, size=(1, 1, (4 * NC) // 4)), 4, axis=2)
    b = rng.integers(-1, 2, size=(N, 128, 4 * NC)) * size
    return {"a": a.reshape(N, 128, 4 * 512).astype(BF), "b": b.astype(np.float32).astype(BF)}
def reference(a, b):
    T = [term(a[r], mx_ref.quantize(b[r])) for r in range(N)]
    y = np.zeros((N, 128, 4 * M), np.float32)
    for c in range(N):
        y[c] = mx_ref.total([cut(T[r], c, 4 * M) for r in range(N)])
    return {"y": y}

import numpy as np
import math
from concourse.bass import DstId, RemoteDMATransfer
from concourse.mybir import dt, AluOpType, ActivationFunctionType

N = 8
PW = 16
SCRATCH = {
    "bt": ("sbuf", [128, 512], "bfloat16"),
    "at": ("sbuf", [128, 2048], "bfloat16"),
    "bq": ("sbuf", [128, 128], "float8_e4m3fn_x4"),
    "bs": ("sbuf", [128, 128], "uint8"),
    "aq": ("sbuf", [128, 512], "float8_e4m3fn_x4"),
    "asc": ("sbuf", [128, 512], "uint8"),
    "ps": ("psum", [128, 2048], "float32"),
    "pd": ("psum", [128, 2048], "float32"),
    "tt": ("sbuf", [128, 512], "bfloat16"),
    "tq": ("sbuf", [128, 128], "float8_e4m3fn_x4"),
    "ts": ("sbuf", [128, 128], "uint8"),
    "ones": ("sbuf", [128, 516], "bfloat16"),
    "zc": ("sbuf", [128, 516], "bfloat16"),
    "wq": ("sbuf", [128, 512], "float8_e4m3fn_x4"),
    "ws": ("sbuf", [128, 512], "uint8"),
    "rq": ("sbuf", [128, 128], "float8_e4m3fn_x4"),
    "rs": ("sbuf", [128, 128], "uint8"),
    "lq": ("sbuf", [128, 32], "float8_e4m3fn_x4"),
    "lp": ("sbuf", [128, 128], "uint8"),
    "tmp": ("sbuf", [128, 256], "float32"),
    "u": ("sbuf", [128, 256], "float32"),
    "z": ("sbuf", [128, 128], "float32"),
    "yt": ("sbuf", [128, 64], "float32"),
}
SEMAPHORES = (["ones", "sel", "ldb", "qb", "qt", "qw", "arr", "land", "sent", "hh", "yd", "st"]
              + ["%s%d" % (n, i) for n in ("lda", "qa", "m", "c", "d", "e", "f") for i in range(4)])

_CACHE = {}


def _bits(mask):
    return [e for e in range(16) if (mask >> e) & 1]


def _deal(allowed):
    free = set(range(16))
    out = [0] * len(allowed)
    for a in sorted(set(allowed), key=lambda m: len(_bits(m))):
        idx = [i for i in range(len(allowed)) if allowed[i] == a]
        pool = [e for e in _bits(a) if e in free]
        n = 1
        while n * 2 * len(idx) <= len(pool):
            n *= 2
        for k, i in enumerate(idx):
            mine = pool[k * n:(k + 1) * n]
            for e in mine:
                free.discard(e)
                out[i] |= 1 << e
    return out


def _plan(cores, topo):
    world = range((1 + max(topo.host(c) for c in cores)) * topo.CORES_PER_HOST)
    hosts = sorted(set(topo.host(c) for c in cores))
    roles = []
    for r, R in enumerate(cores):
        h = topo.host(R)
        group = {k: [i for i, c in enumerate(cores) if topo.host(c) == k] for k in hosts}
        far = {k: [cores[i] for i in group[k] if cores[i] != R and not topo.may_write(R, cores[i])] for k in hosts}
        rackh = [k for k in hosts if k != h and topo.rack(k) == topo.rack(h)][0]
        others = [k for k in hosts if topo.rack(k) != topo.rack(h)]
        diag = [k for k in others if len(far[k]) == len(group[k])][0]
        cable = [k for k in others if k != diag][0]
        key = lambda x: (topo.die(x) != topo.die(R), x)
        home = sorted([x for x in world if x != R and topo.host(x) == h and topo.chip(x) == topo.chip(R)
                       and topo.may_write(x, far[h][0])], key=key)
        gate = sorted([x for x in world if topo.same_plane(R, x) and topo.mates(x, far[rackh][0])
                       and topo.may_write(x, far[rackh][0])], key=key)
        for place, pair in ((home, (h, cable)), (gate, (rackh, diag))):
            for n, (kind, k) in enumerate((("c", pair[0]), ("c", pair[1]), ("p", pair[0]), ("p", pair[1]))):
                roles.append((r, kind, min(group[k]), place[n]))
    send, fwd, arrive = {}, {}, [0] * len(cores)
    for r, R in enumerate(cores):
        mine = [ro for ro in roles if ro[0] == r]
        masks = _deal([topo.mask(R, ro[3]) for ro in mine])
        send[R] = list(zip(mine, masks))
        for ro, mk in zip(mine, masks):
            x = ro[3]
            dests = [ro[2], ro[2] + 1]
            fm = _deal([topo.mask(x, cores[d]) for d in dests])
            fwd[x] = (ro, len(_bits(mk)), list(zip(dests, fm)))
            for d, m in zip(dests, fm):
                arrive[d] += len(_bits(m))
    return send, fwd, arrive


def _dst(topo, d, src):
    rid, pid = topo.addr(d, src)
    return [DstId(rid=rid, pnc=pid)]


def rank_program(g, core, T, topo):
    if "p" not in _CACHE:
        _CACHE["p"] = _plan(list(T.cores), topo)
    send, fwd, arrive = _CACHE["p"]
    S = T.sem
    u8 = dt.uint8

    if core in fwd:
        (r, kind, lo, _x), n_in, jobs = fwd[core]
        g.wait_ge(S.land, n_in)
        tr = []
        for d, mk in jobs:
            if kind == "c":
                o = (d - lo) * PW
                src = T.lq[:, o:o + PW].bitcast(u8)
                dst = T.rq[:, r * PW:(r + 1) * PW].bitcast(u8)
            else:
                src = T.lp[:, d * PW:(d + 1) * PW]
                dst = T.rs[:, r * PW:(r + 1) * PW]
            tr.append(RemoteDMATransfer(dst_ids=_dst(topo, T.cores[d], core), dma_engine_mask=mk, remote_sem=S.arr,
                                        src=src, dst=dst))
        g.remote_dma_fused(tr, local_sem=S.sent)
        g.wait_ge(S.sent, sum(len(_bits(mk)) for _d, mk in jobs))
        return

    rank = T.rank_of(core)
    if rank is None:
        return
    V, P, A, Y = g.vector, g.tensor, g.scalar, g.sync
    add = AluOpType.add
    Copy = ActivationFunctionType.Copy

    Y.dma_start(T.bt[:], T.b[:]).then_inc(S.ldb, 16)
    for i in range(4):
        q = A if i % 2 == 0 else Y
        q.dma_start(T.at[:, 512 * i:512 * i + 512], T.a[:, 512 * i:512 * i + 512]).then_inc(S["lda%d" % i], 16)

    V.memset(T.ones[:], 1.0).then_inc(S.ones, 1)
    g.wait_ge(S.ones, 1)
    g.affine_select(T.zc[:], T.ones[:], [[1, 516]], AluOpType.is_equal, 0.0, -3, -4).then_inc(S.sel, 1)

    V.wait_ge(S.ldb, 16)
    V.quantize_mx(T.bq[:], T.bs[:], T.bt[:]).then_inc(S.qb, 1)
    P.wait_ge(S.qb, 1)
    for i in range(4):
        c0, c1 = 128 * i, 128 * i + 128
        V.wait_ge(S["lda%d" % i], 16)
        V.quantize_mx(T.aq[:, c0:c1], T.asc[:, c0:c1], T.at[:, 512 * i:512 * i + 512]).then_inc(S["qa%d" % i], 1)
        P.wait_ge(S["qa%d" % i], 1)
        P.matmul_mx(T.ps[:, 512 * i:512 * i + 128], T.aq[:, c0:c1], T.asc[:, c0:c1], T.bq[:], T.bs[:],
                    True, True).then_inc(S["m%d" % i], 1)
        if i < 3:
            A.wait_ge(S["m%d" % i], 1)
            A.activation(T.tt[:, i:512:4], T.ps[:, 512 * i:512 * i + 128], Copy).then_inc(S["c%d" % i], 1)
    V.wait_ge(S.m3, 1)
    V.tensor_copy(T.tt[:, 3:512:4], T.ps[:, 1536:1664]).then_inc(S.c3, 1)
    for i in range(4):
        V.wait_ge(S["c%d" % i], 1)
    V.quantize_mx(T.tq[:], T.ts[:], T.tt[:]).then_inc(S.qt, 1)

    g.wait_ge(S.qt, 1)
    tr = []
    for (r, kind, lo, x), mk in send[core]:
        if kind == "c":
            src = T.tq[:, lo * PW:(lo + 2) * PW].bitcast(u8)
            dst = T.lq[:].bitcast(u8)
        else:
            src = T.ts[:]
            dst = T.lp[:]
        tr.append(RemoteDMATransfer(dst_ids=_dst(topo, x, core), dma_engine_mask=mk, remote_sem=S.land, src=src, dst=dst))
    g.remote_dma_fused(tr, local_sem=S.sent)

    V.wait_ge(S.sel, 1)
    for t in range(4):
        V.quantize_mx(T.wq[:, 128 * t:128 * t + 128], T.ws[:, 128 * t:128 * t + 128],
                      T.zc[:, 3 - t:3 - t + 512]).then_inc(S.qw, 1)
    P.wait_ge(S.qw, 4)

    P.wait_ge(S.arr, arrive[rank])
    for t in range(4):
        b0 = 512 * t
        P.matmul_mx(T.pd[:, b0:b0 + 128], T.wq[:, 128 * t:128 * t + 128], T.ws[:, 128 * t:128 * t + 128],
                    T.rq[:], T.rs[:], True, True).then_inc(S["d%d" % t], 1)
        A.wait_ge(S["d%d" % t], 1)
        A.activation(T.tmp[:, 64 * t:64 * t + 64], T.pd[:, b0 + 64:b0 + 128], Copy).then_inc(S["e%d" % t], 1)
        V.wait_ge(S["e%d" % t], 1)
        V.tensor_tensor(T.u[:, 64 * t:64 * t + 64], T.pd[:, b0:b0 + 64], T.tmp[:, 64 * t:64 * t + 64],
                        add).then_inc(S["f%d" % t], 1)
        V.wait_ge(S["f%d" % t], 1)
        V.tensor_tensor(T.z[:, t:128:4], T.u[:, 64 * t:64 * t + 32], T.u[:, 64 * t + 32:64 * t + 64],
                        add).then_inc(S.hh, 1)
    V.wait_ge(S.hh, 4)
    V.tensor_tensor(T.yt[:], T.z[:, 0:64], T.z[:, 64:128], add).then_inc(S.yd, 1)
    Y.wait_ge(S.yd, 1)
    Y.dma_start(T.y[:], T.yt[:]).then_inc(S.st, 16)
    Y.wait_ge(S.st, 16)
    g.wait_ge(S.sent, sum(len(_bits(mk)) for _ro, mk in send[core]))
